import numpy as np
import ml_dtypes


def mxq(x, axis, fmt="e4m3"):
    dtype, down = {"e4m3": (ml_dtypes.float8_e4m3fn, 7), "e5m2": (ml_dtypes.float8_e5m2, 14)}[fmt]
    v = np.moveaxis(np.asarray(x, np.float32).astype(ml_dtypes.bfloat16).astype(np.float64), axis, -1)
    blocks = v.reshape(v.shape[:-1] + (-1, 32))
    amax = np.abs(blocks).max(-1, keepdims=True)
    byte = np.maximum(np.where(amax > 0, np.frexp(amax)[1] - 1 + 127, 0) - down, 1)
    scale = np.exp2(byte - 127.0)
    codes = (blocks / scale).astype(np.float32).astype(dtype).astype(np.float64)
    return np.moveaxis((codes * scale).reshape(v.shape), -1, axis)


WIDE = False


def mx_kscale(k):
    if not WIDE:
        return np.ones(k)
    levels = np.array([10, -10, 5, -5, 0])
    if k % 512:
        return np.exp2(np.random.permutation(np.resize(levels, k // 32))).repeat(32)
    a = np.empty((k // 512, 16))
    for p in range(k // 512):
        a[p, :8] = np.random.permutation(np.resize(levels, 8))
        for g in range(8):
            far = levels[np.abs(levels - a[p, g]) >= 10]
            a[p, g + 8] = far[np.random.randint(len(far))]
    return np.exp2(a.ravel()).repeat(32)


def f64(x):
    return np.asarray(x).astype(np.float64)


def striped(idx):
    return np.tile(idx.reshape(-1, 16).T, (8, 1)).astype(np.uint16)


def unstriped(offs):
    return offs[:16].T.reshape(-1).astype(np.int64)


def pack_weight(w):
    k, n = w.shape
    w = f64(np.asarray(w, np.float32).astype(ml_dtypes.bfloat16)).reshape(k // 32, 32, n)
    amax = np.abs(w).max(1)
    byte = np.clip(np.where(amax > 0, np.frexp(amax)[1] - 1 + 127 - 7, 1), 1, 254)
    scaled = (w * np.exp2(127.0 - byte)[:, None, :]).reshape(k, n).astype(np.float32)
    words = np.ascontiguousarray(scaled.reshape(k // 512, 128, 4, n).transpose(0, 1, 3, 2)).astype(ml_dtypes.float8_e4m3fn).view(np.uint8)
    return words, np.ascontiguousarray(byte.astype(np.uint8).reshape(k // 512, 16, n))


def unpack_weight(words, scales):
    g, p, n, _ = words.shape
    vals = np.ascontiguousarray(words).view(ml_dtypes.float8_e4m3fn).astype(np.float64) * np.repeat(np.exp2(scales.astype(np.float64) - 127.0), 8, axis=1)[..., None]
    return vals.transpose(0, 1, 3, 2).reshape(g * 512, n)


K, T, E, C, N = 1024, 768, 6, 256, 256


def by_expert(wq, xq):
    return np.concatenate([wq[e].T @ xq[:, e * C:(e + 1) * C] for e in range(E)], axis=1)


def setup_inputs():
    n = np.random.standard_normal
    s = mx_kscale(K)[:, None]
    first = np.random.permutation(np.repeat(np.arange(E), T // E))
    second = (first + 1 + np.random.permutation(np.repeat(np.arange(E - 1), -(-T // (E - 1)))[:T])) % E
    while np.bincount(second, minlength=E).max() != T // E:
        load = np.bincount(second, minlength=E); hi, lo = int(load.argmax()), int(load.argmin())
        t = np.flatnonzero((second == hi) & (first != lo))[0]; second[t] = lo
    slot_token = np.empty(E * C, np.int64); pos = np.empty((2, T), np.int64); fill = np.zeros(E, np.int64)
    place = np.stack([np.random.permutation(C) for _ in range(E)])
    for r, deal in enumerate((first, second)):
        for t in np.random.permutation(T):
            e = deal[t]; j = e * C + place[e, fill[e]]; fill[e] += 1; slot_token[j] = t; pos[r, t] = j
    g = np.random.uniform(0.2, 0.8, T)
    packed = [pack_weight(m) for m in n((E, K, N)) / np.sqrt(K) / s[None]]
    return {
        "xT": (n((K, T)) * s).astype(np.float32),
        "w_words": np.stack([m[0] for m in packed]),
        "w_scales": np.stack([m[1] for m in packed]),
        "b": (0.3 * n((N, E))).astype(np.float32),
        "gate": np.stack([np.tile(g, (N, 1)), np.tile(1.0 - g, (N, 1))]).astype(np.float32),
        "offs": striped(slot_token),
        "pos1": striped(pos[0]),
        "pos2": striped(pos[1]),
    }


def reference(xT, w_words, w_scales, b, gate, offs, pos1, pos2):
    idx = unstriped(offs)
    xq = mxq(f64(xT)[:, idx], 0, "e4m3")
    w = np.stack([unpack_weight(w_words[e], w_scales[e]) for e in range(E)])
    y = by_expert(w, xq)
    y = y + np.repeat(f64(b), C, axis=1)
    return f64(gate[0]) * y[:, unstriped(pos1)] + f64(gate[1]) * y[:, unstriped(pos2)]

@@ -1,0 +1,122 @@
+from contextlib import ExitStack
+
+import concourse.mybir as mybir
+
+K, T, E, C, N = 1024, 768, 6, 256, 256
+FLOPS = 2 * K * N * E * C
+P = 128
+PASSES = 2
+BLOCKS = 2
+SLOTS = E * C
+
+F32 = mybir.dt.float32
+BF16 = mybir.dt.bfloat16
+U32 = mybir.dt.uint32
+I32 = mybir.dt.int32
+U16 = mybir.dt.uint16
+U8 = mybir.dt.uint8
+FP8X4 = mybir.dt.float8_e4m3fn_x4
+MULT = mybir.AluOpType.mult
+ADD = mybir.AluOpType.add
+IDENTITY = mybir.ActivationFunctionType.Identity
+
+CHUNKS = ((0, 512), (512, 256))
+SCALAR_COLS = {(0, 0): 192, (0, 512): 128, (1, 0): 512, (1, 512): 128}
+GATHER = 512
+
+
+def interleave(copy, grouped, raw, lo, hi):
+    if hi > lo:
+        copy(
+            grouped[:, lo:hi, :].rearrange("p (c i) t -> p c t i", i=4),
+            raw[:, :, lo:hi].rearrange("p t (c i) -> p c t i", i=4),
+        )
+
+
+def tile_routed_moe_kernel(tc, xT, w_words, w_scales, b, gate, offs, pos1, pos2, out):
+    nc = tc.nc
+    with ExitStack() as ctx:
+        keep = ctx.enter_context(tc.tile_pool(name="keep", bufs=1))
+        psum = ctx.enter_context(tc.psum_pool(name="psum", bufs=6))
+
+        offs_sb = keep.tile([P, SLOTS // 16], U16)
+        pos1_sb = keep.tile([P, T // 16], U16)
+        pos2_sb = keep.tile([P, T // 16], U16)
+        bias = keep.tile([P, BLOCKS, E], F32)
+        gates = keep.tile([P, 2, T], F32)
+        w_codes = keep.tile([P, E, PASSES, 4 * N], U8, align_bytes=64)
+        w_planes = keep.tile([P, E * PASSES, N], U8, align_bytes=64)
+        x_planes = keep.tile([P, T], U8, align_bytes=64)
+        s_planes = keep.tile([P, SLOTS], U8, align_bytes=64)
+        x_codes = [keep.tile([P, T], U32, align_bytes=64, name=f"x_codes{a}") for a in range(PASSES)]
+        s_codes = [keep.tile([P, SLOTS], U32, align_bytes=64, name=f"s_codes{a}") for a in range(PASSES)]
+        y = [keep.tile([P, SLOTS], F32, name=f"y{n}") for n in range(BLOCKS)]
+
+        nc.gpsimd.memset(x_planes[:], 0)
+        nc.vector.memset(w_planes[:].rearrange("p g n -> p (g n)").bitcast(I32), 0)
+
+        x_rows = xT.rearrange("(a p t) n -> a p t n", p=P, t=4)
+        raw = {}
+        for a in range(PASSES):
+            for lo, n in CHUNKS:
+                raw[a, lo] = keep.tile([P, 4, n], F32, name=f"raw{a}_{lo}")
+                nc.sync.dma_start(out=raw[a, lo][:], in_=x_rows[a, :, :, lo : lo + n])
+            if a == 0:
+                nc.sync.dma_start(offs_sb[:], offs)
+        for r in range(4):
+            nc.sync.dma_start(
+                out=w_planes[r : P : 32, :, :].bitcast(I32),
+                in_=w_scales.rearrange("e a (q r) n -> r q (e a) n", r=4)[r].bitcast(I32),
+            )
+        for e in range(0, E, 2):
+            nc.sync.dma_start(
+                out=w_codes[:, e : e + 2, :, :].rearrange("p e a n -> p (e a) n"),
+                in_=w_words[e : e + 2].rearrange("e a p n t -> p (e a) (n t)"),
+            )
+        nc.scalar.dma_start(out=bias[:], in_=b.rearrange("(c p) e -> p c e", p=P))
+        nc.sync.dma_start(pos1_sb[:], pos1)
+        nc.sync.dma_start(pos2_sb[:], pos2)
+        nc.sync.dma_start(out=gates[:], in_=gate[:, 0:P, :].rearrange("g p n -> p g n"))
+
+        for a in range(PASSES):
+            for lo, n in CHUNKS:
+                grouped = keep.tile([P, n, 4], BF16, align_bytes=64, name=f"grouped{a}_{lo}")
+                cut = SCALAR_COLS[a, lo]
+                interleave(nc.scalar.copy, grouped, raw[a, lo], 0, cut)
+                interleave(nc.vector.tensor_copy, grouped, raw[a, lo], cut, n)
+                nc.vector.quantize_mx(
+                    out=x_codes[a][:, lo : lo + n].bitcast(FP8X4),
+                    scales=x_planes[4 * a : P, lo : lo + n],
+                    in_=grouped[:].rearrange("p n t -> p (n t)"),
+                )
+            if a == 0:
+                for s in range(0, SLOTS, GATHER):
+                    nc.vector.tensor_copy(s_codes[0][:, s : s + GATHER], x_codes[0][:].indirect(offs_sb[:, s // 16 : (s + GATHER) // 16]))
+        for s in range(0, SLOTS, GATHER):
+            nc.vector.tensor_copy(s_planes[:, s : s + GATHER], x_planes[:].indirect(offs_sb[:, s // 16 : (s + GATHER) // 16]))
+        for s in range(0, SLOTS, GATHER):
+            nc.vector.tensor_copy(s_codes[1][:, s : s + GATHER], x_codes[1][:].indirect(offs_sb[:, s // 16 : (s + GATHER) // 16]))
+            for e in range(s // C, (s + GATHER) // C):
+                cols = slice(e * C, (e + 1) * C)
+                acc = psum.tile([P, BLOCKS, C], F32)
+                for n in range(BLOCKS):
+                    for a in range(PASSES):
+                        nc.tensor.matmul_mx(
+                            out=acc[:, n, :],
+                            lhsT=w_codes[:, e, a, n * 512 : (n + 1) * 512].bitcast(FP8X4),
+                            lhsT_scale=w_planes[:, e * PASSES + a, n * P : (n + 1) * P],
+                            rhs=s_codes[a][:, cols].bitcast(FP8X4),
+                            rhs_scale=s_planes[4 * a : P, cols],
+                            start=(a == 0),
+                            stop=(a == PASSES - 1),
+                        )
+                    nc.scalar.activation(y[n][:, cols], acc[:, n, :], IDENTITY, bias=bias[:, n, e : e + 1])
+
+        for n, lo, hi in ((0, 0, 768), (1, 0, 512), (1, 512, 768)):
+            first = keep.tile([P, hi - lo], F32, name=f"first{n}_{lo}")
+            second = keep.tile([P, hi - lo], F32, name=f"second{n}_{lo}")
+            total = keep.tile([P, hi - lo], F32, name=f"total{n}_{lo}")
+            nc.vector.tensor_tensor(first[:], y[n][:].indirect(pos1_sb[:, lo // 16 : hi // 16]), gates[:, 0, lo:hi], MULT)
+            nc.vector.tensor_tensor(second[:], y[n][:].indirect(pos2_sb[:, lo // 16 : hi // 16]), gates[:, 1, lo:hi], MULT)
+            nc.vector.tensor_tensor(total[:], first[:], second[:], ADD)
+            nc.sync.dma_start(out=out[n * P : (n + 1) * P, lo:hi], in_=total[:])

@@ -20,8 +20,8 @@ MULT = mybir.AluOpType.mult
 ADD = mybir.AluOpType.add
 IDENTITY = mybir.ActivationFunctionType.Identity
 
-CHUNKS = ((0, 512), (512, 256))
-SCALAR_COLS = {(0, 0): 192, (0, 512): 128, (1, 0): 512, (1, 512): 128}
+CHUNKS = ((0, 256), (256, 256), (512, 256))
+SCALAR_COLS = {(0, 0): 0, (0, 256): 256, (0, 512): 64, (1, 0): 256, (1, 256): 256, (1, 512): 256}
 GATHER = 512
 
 
@@ -37,7 +37,7 @@ def tile_routed_moe_kernel(tc, xT, w_words, w_scales, b, gate, offs, pos1, pos2,
     nc = tc.nc
     with ExitStack() as ctx:
         keep = ctx.enter_context(tc.tile_pool(name="keep", bufs=1))
-        psum = ctx.enter_context(tc.psum_pool(name="psum", bufs=6))
+        psum = ctx.enter_context(tc.psum_pool(name="psum", bufs=8))
 
         offs_sb = keep.tile([P, SLOTS // 16], U16)
         pos1_sb = keep.tile([P, T // 16], U16)
@@ -48,7 +48,6 @@ def tile_routed_moe_kernel(tc, xT, w_words, w_scales, b, gate, offs, pos1, pos2,
         w_planes = keep.tile([P, E * PASSES, N], U8, align_bytes=64)
         x_planes = keep.tile([P, T], U8, align_bytes=64)
         s_planes = keep.tile([P, SLOTS], U8, align_bytes=64)
-        x_codes = [keep.tile([P, T], U32, align_bytes=64, name=f"x_codes{a}") for a in range(PASSES)]
         s_codes = [keep.tile([P, SLOTS], U32, align_bytes=64, name=f"s_codes{a}") for a in range(PASSES)]
         y = [keep.tile([P, SLOTS], F32, name=f"y{n}") for n in range(BLOCKS)]
 
@@ -79,38 +78,50 @@ def tile_routed_moe_kernel(tc, xT, w_words, w_scales, b, gate, offs, pos1, pos2,
         nc.sync.dma_start(out=gates[:], in_=gate[:, 0:P, :].rearrange("g p n -> p g n"))
 
         for a in range(PASSES):
+            x_codes = keep.tile([P, T], U32, align_bytes=64)
             for lo, n in CHUNKS:
                 grouped = keep.tile([P, n, 4], BF16, align_bytes=64, name=f"grouped{a}_{lo}")
                 cut = SCALAR_COLS[a, lo]
                 interleave(nc.scalar.copy, grouped, raw[a, lo], 0, cut)
                 interleave(nc.vector.tensor_copy, grouped, raw[a, lo], cut, n)
                 nc.vector.quantize_mx(
-                    out=x_codes[a][:, lo : lo + n].bitcast(FP8X4),
+                    out=x_codes[:, lo : lo + n].bitcast(FP8X4),
                     scales=x_planes[4 * a : P, lo : lo + n],
                     in_=grouped[:].rearrange("p n t -> p (n t)"),
                 )
             if a == 0:
                 for s in range(0, SLOTS, GATHER):
-                    nc.vector.tensor_copy(s_codes[0][:, s : s + GATHER], x_codes[0][:].indirect(offs_sb[:, s // 16 : (s + GATHER) // 16]))
-        for s in range(0, SLOTS, GATHER):
-            nc.vector.tensor_copy(s_planes[:, s : s + GATHER], x_planes[:].indirect(offs_sb[:, s // 16 : (s + GATHER) // 16]))
-        for s in range(0, SLOTS, GATHER):
-            nc.vector.tensor_copy(s_codes[1][:, s : s + GATHER], x_codes[1][:].indirect(offs_sb[:, s // 16 : (s + GATHER) // 16]))
-            for e in range(s // C, (s + GATHER) // C):
-                cols = slice(e * C, (e + 1) * C)
-                acc = psum.tile([P, BLOCKS, C], F32)
+                    nc.vector.tensor_copy(s_codes[0][:, s : s + GATHER], x_codes[:].indirect(offs_sb[:, s // 16 : (s + GATHER) // 16]))
+        def gather(slots, tokens, lo, hi):
+            nc.vector.tensor_copy(slots[:, lo:hi], tokens[:].indirect(offs_sb[:, lo // 16 : hi // 16]))
+
+        def multiply(e):
+            cols = slice(e * C, (e + 1) * C)
+            accs = [psum.tile([P, C], F32, name="acc") for n in range(BLOCKS)]
+            for a in range(PASSES):
                 for n in range(BLOCKS):
-                    for a in range(PASSES):
-                        nc.tensor.matmul_mx(
-                            out=acc[:, n, :],
-                            lhsT=w_codes[:, e, a, n * 512 : (n + 1) * 512].bitcast(FP8X4),
-                            lhsT_scale=w_planes[:, e * PASSES + a, n * P : (n + 1) * P],
-                            rhs=s_codes[a][:, cols].bitcast(FP8X4),
-                            rhs_scale=s_planes[4 * a : P, cols],
-                            start=(a == 0),
-                            stop=(a == PASSES - 1),
-                        )
-                    nc.scalar.activation(y[n][:, cols], acc[:, n, :], IDENTITY, bias=bias[:, n, e : e + 1])
+                    nc.tensor.matmul_mx(
+                        out=accs[n][:],
+                        lhsT=w_codes[:, e, a, n * 512 : (n + 1) * 512].bitcast(FP8X4),
+                        lhsT_scale=w_planes[:, e * PASSES + a, n * P : (n + 1) * P],
+                        rhs=s_codes[a][:, cols].bitcast(FP8X4),
+                        rhs_scale=s_planes[4 * a : P, cols],
+                        start=(a == 0),
+                        stop=(a == PASSES - 1),
+                    )
+            for n in range(BLOCKS):
+                nc.scalar.activation(y[n][:, cols], accs[n][:], IDENTITY, bias=bias[:, n, e : e + 1])
+
+        for first in range(0, E, 2):
+            lo, mid, hi = first * C, (first + 1) * C, (first + 2) * C
+            gather(s_planes, x_planes, lo, hi)
+            if first + 2 < E:
+                gather(s_codes[1], x_codes, lo, hi)
+            else:
+                gather(s_codes[1], x_codes, lo, mid)
+                gather(s_codes[1], x_codes, mid, hi)
+            multiply(first)
+            multiply(first + 1)
 
         for n, lo, hi in ((0, 0, 768), (1, 0, 512), (1, 512, 768)):
             first = keep.tile([P, hi - lo], F32, name=f"first{n}_{lo}")

@@ -1,6 +1,7 @@
 from contextlib import ExitStack
 
 import concourse.mybir as mybir
+from concourse.masks import make_identity
 
 K, T, E, C, N = 1024, 768, 6, 256, 256
 FLOPS = 2 * K * N * E * C
@@ -21,7 +22,7 @@ ADD = mybir.AluOpType.add
 IDENTITY = mybir.ActivationFunctionType.Identity
 
 CHUNKS = ((0, 256), (256, 256), (512, 256))
-SCALAR_COLS = {(0, 0): 0, (0, 256): 256, (0, 512): 64, (1, 0): 256, (1, 256): 256, (1, 512): 256}
+SCALAR_COLS = {(0, 0): 88, (0, 256): 88, (0, 512): 88, (1, 0): 256, (1, 256): 256, (1, 512): 256}
 GATHER = 512
 
 
@@ -52,6 +53,8 @@ def tile_routed_moe_kernel(tc, xT, w_words, w_scales, b, gate, offs, pos1, pos2,
         y = [keep.tile([P, SLOTS], F32, name=f"y{n}") for n in range(BLOCKS)]
 
         nc.gpsimd.memset(x_planes[:], 0)
+        ident = keep.tile([P, P], F32)
+        make_identity(nc, ident[:])
         nc.vector.memset(w_planes[:].rearrange("p g n -> p (g n)").bitcast(I32), 0)
 
         x_rows = xT.rearrange("(a p t) n -> a p t n", p=P, t=4)
@@ -97,11 +100,11 @@ def tile_routed_moe_kernel(tc, xT, w_words, w_scales, b, gate, offs, pos1, pos2,
 
         def multiply(e):
             cols = slice(e * C, (e + 1) * C)
-            accs = [psum.tile([P, C], F32, name="acc") for n in range(BLOCKS)]
+            accs = [psum.tile([P, 512], F32, name="acc") for n in range(BLOCKS)]
             for a in range(PASSES):
                 for n in range(BLOCKS):
                     nc.tensor.matmul_mx(
-                        out=accs[n][:],
+                        out=accs[n][:, 0:C],
                         lhsT=w_codes[:, e, a, n * 512 : (n + 1) * 512].bitcast(FP8X4),
                         lhsT_scale=w_planes[:, e * PASSES + a, n * P : (n + 1) * P],
                         rhs=s_codes[a][:, cols].bitcast(FP8X4),
@@ -110,7 +113,7 @@ def tile_routed_moe_kernel(tc, xT, w_words, w_scales, b, gate, offs, pos1, pos2,
                         stop=(a == PASSES - 1),
                     )
             for n in range(BLOCKS):
-                nc.scalar.activation(y[n][:, cols], accs[n][:], IDENTITY, bias=bias[:, n, e : e + 1])
+                nc.scalar.activation(y[n][:, cols], accs[n][:, 0:C], IDENTITY, bias=bias[:, n, e : e + 1])
 
         for first in range(0, E, 2):
             lo, mid, hi = first * C, (first + 1) * C, (first + 2) * C
@@ -123,11 +126,27 @@ def tile_routed_moe_kernel(tc, xT, w_words, w_scales, b, gate, offs, pos1, pos2,
             multiply(first)
             multiply(first + 1)
 
-        for n, lo, hi in ((0, 0, 768), (1, 0, 512), (1, 512, 768)):
-            first = keep.tile([P, hi - lo], F32, name=f"first{n}_{lo}")
-            second = keep.tile([P, hi - lo], F32, name=f"second{n}_{lo}")
-            total = keep.tile([P, hi - lo], F32, name=f"total{n}_{lo}")
-            nc.vector.tensor_tensor(first[:], y[n][:].indirect(pos1_sb[:, lo // 16 : hi // 16]), gates[:, 0, lo:hi], MULT)
-            nc.vector.tensor_tensor(second[:], y[n][:].indirect(pos2_sb[:, lo // 16 : hi // 16]), gates[:, 1, lo:hi], MULT)
-            nc.vector.tensor_tensor(total[:], first[:], second[:], ADD)
-            nc.sync.dma_start(out=out[n * P : (n + 1) * P, lo:hi], in_=total[:])
+        def fetch(into, n, positions, weight, lo, hi):
+            nc.vector.tensor_tensor(into[:, lo:hi], y[n][:].indirect(positions[:, lo // 16 : hi // 16]), gates[:, weight, lo:hi], MULT)
+
+        first = [keep.tile([P, T], F32, name=f"first{n}") for n in range(BLOCKS)]
+        second = [keep.tile([P, T], F32, name=f"second{n}") for n in range(BLOCKS)]
+        total = [keep.tile([P, T], F32, name=f"total{n}") for n in range(BLOCKS)]
+        both = psum.tile([P, 512], F32, name="acc")
+
+        def add(n, lo, hi):
+            nc.vector.tensor_tensor(total[n][:, lo:hi], first[n][:, lo:hi], second[n][:, lo:hi], ADD)
+            nc.sync.dma_start(out=out[n * P : (n + 1) * P, lo:hi], in_=total[n][:, lo:hi])
+
+        fetch(first[0], 0, pos1_sb, 0, 0, T)
+        nc.tensor.matmul(both[:], ident[:], first[0][:, 0:512], start=True, stop=False)
+        fetch(second[0], 0, pos2_sb, 1, 0, T)
+        nc.tensor.matmul(both[:], ident[:], second[0][:, 0:512], start=False, stop=True)
+        fetch(first[1], 1, pos1_sb, 0, 0, T)
+        add(0, 512, T)
+        nc.scalar.copy(total[0][:, 0:512], both[:])
+        nc.sync.dma_start(out=out[0:P, 0:512], in_=total[0][:, 0:512])
+        fetch(second[1], 1, pos2_sb, 1, 0, 512)
+        fetch(second[1], 1, pos2_sb, 1, 512, T)
+        add(1, 0, 512)
+        add(1, 512, T)

@@ -21,15 +21,15 @@ MULT = mybir.AluOpType.mult
 ADD = mybir.AluOpType.add
 IDENTITY = mybir.ActivationFunctionType.Identity
 
-CHUNKS = ((0, 256), (256, 256), (512, 256))
-SCALAR_COLS = {(0, 0): 88, (0, 256): 88, (0, 512): 88, (1, 0): 256, (1, 256): 256, (1, 512): 256}
+CHUNKS = (((0, 256, 88), (256, 256, 88), (512, 128, 44), (640, 128, 44)), ((0, 256, 256), (256, 256, 256), (512, 256, 256)))
+QUANT = (((0, 256), (256, 256), (512, 128), (640, 128)), ((0, 512), (512, 256)))
 GATHER = 512
 
 
-def interleave(copy, grouped, raw, lo, hi):
+def interleave(copy, grouped, raw, lo, hi, base):
     if hi > lo:
         copy(
-            grouped[:, lo:hi, :].rearrange("p (c i) t -> p c t i", i=4),
+            grouped[:, lo + base : hi + base, :].rearrange("p (c i) t -> p c t i", i=4),
             raw[:, :, lo:hi].rearrange("p t (c i) -> p c t i", i=4),
         )
 
@@ -60,7 +60,7 @@ def tile_routed_moe_kernel(tc, xT, w_words, w_scales, b, gate, offs, pos1, pos2,
         x_rows = xT.rearrange("(a p t) n -> a p t n", p=P, t=4)
         raw = {}
         for a in range(PASSES):
-            for lo, n in CHUNKS:
+            for lo, n, share in CHUNKS[a]:
                 raw[a, lo] = keep.tile([P, 4, n], F32, name=f"raw{a}_{lo}")
                 nc.sync.dma_start(out=raw[a, lo][:], in_=x_rows[a, :, :, lo : lo + n])
             if a == 0:
@@ -80,23 +80,24 @@ def tile_routed_moe_kernel(tc, xT, w_words, w_scales, b, gate, offs, pos1, pos2,
         nc.sync.dma_start(pos2_sb[:], pos2)
         nc.sync.dma_start(out=gates[:], in_=gate[:, 0:P, :].rearrange("g p n -> p g n"))
 
+        def gather(slots, tokens, lo, hi):
+            nc.vector.tensor_copy(slots[:, lo:hi], tokens[:].indirect(offs_sb[:, lo // 16 : hi // 16]))
+
         for a in range(PASSES):
-            x_codes = keep.tile([P, T], U32, align_bytes=64)
-            for lo, n in CHUNKS:
-                grouped = keep.tile([P, n, 4], BF16, align_bytes=64, name=f"grouped{a}_{lo}")
-                cut = SCALAR_COLS[a, lo]
-                interleave(nc.scalar.copy, grouped, raw[a, lo], 0, cut)
-                interleave(nc.vector.tensor_copy, grouped, raw[a, lo], cut, n)
+            x_codes = keep.tile([P, T], U32, align_bytes=64, name=f"x_codes{a}")
+            grouped = keep.tile([P, T, 4], BF16, align_bytes=64, name=f"grouped{a}")
+            for lo, n, share in CHUNKS[a]:
+                interleave(nc.scalar.copy, grouped, raw[a, lo], 0, share, lo)
+                interleave(nc.vector.tensor_copy, grouped, raw[a, lo], share, n, lo)
+            for lo, n in QUANT[a]:
                 nc.vector.quantize_mx(
                     out=x_codes[:, lo : lo + n].bitcast(FP8X4),
                     scales=x_planes[4 * a : P, lo : lo + n],
-                    in_=grouped[:].rearrange("p n t -> p (n t)"),
+                    in_=grouped[:, lo : lo + n, :].rearrange("p n t -> p (n t)"),
                 )
             if a == 0:
                 for s in range(0, SLOTS, GATHER):
-                    nc.vector.tensor_copy(s_codes[0][:, s : s + GATHER], x_codes[:].indirect(offs_sb[:, s // 16 : (s + GATHER) // 16]))
-        def gather(slots, tokens, lo, hi):
-            nc.vector.tensor_copy(slots[:, lo:hi], tokens[:].indirect(offs_sb[:, lo // 16 : hi // 16]))
+                    gather(s_codes[0], x_codes, s, s + GATHER)
 
         def multiply(e):
             cols = slice(e * C, (e + 1) * C)
@@ -132,21 +133,24 @@ def tile_routed_moe_kernel(tc, xT, w_words, w_scales, b, gate, offs, pos1, pos2,
         first = [keep.tile([P, T], F32, name=f"first{n}") for n in range(BLOCKS)]
         second = [keep.tile([P, T], F32, name=f"second{n}") for n in range(BLOCKS)]
         total = [keep.tile([P, T], F32, name=f"total{n}") for n in range(BLOCKS)]
-        both = psum.tile([P, 512], F32, name="acc")
+        pieces = ((0, 320), (320, 640))
+        both = [psum.tile([P, 512], F32, name="acc") for piece in pieces]
 
         def add(n, lo, hi):
             nc.vector.tensor_tensor(total[n][:, lo:hi], first[n][:, lo:hi], second[n][:, lo:hi], ADD)
             nc.sync.dma_start(out=out[n * P : (n + 1) * P, lo:hi], in_=total[n][:, lo:hi])
 
         fetch(first[0], 0, pos1_sb, 0, 0, T)
-        nc.tensor.matmul(both[:], ident[:], first[0][:, 0:512], start=True, stop=False)
+        for acc, (lo, hi) in zip(both, pieces):
+            nc.tensor.matmul(acc[:, 0 : hi - lo], ident[:], first[0][:, lo:hi], start=True, stop=False)
         fetch(second[0], 0, pos2_sb, 1, 0, T)
-        nc.tensor.matmul(both[:], ident[:], second[0][:, 0:512], start=False, stop=True)
+        for acc, (lo, hi) in zip(both, pieces):
+            nc.tensor.matmul(acc[:, 0 : hi - lo], ident[:], second[0][:, lo:hi], start=False, stop=True)
         fetch(first[1], 1, pos1_sb, 0, 0, T)
-        add(0, 512, T)
-        nc.scalar.copy(total[0][:, 0:512], both[:])
-        nc.sync.dma_start(out=out[0:P, 0:512], in_=total[0][:, 0:512])
-        fetch(second[1], 1, pos2_sb, 1, 0, 512)
-        fetch(second[1], 1, pos2_sb, 1, 512, T)
+        for acc, (lo, hi) in zip(both, pieces):
+            nc.scalar.copy(total[0][:, lo:hi], acc[:, 0 : hi - lo])
+            nc.sync.dma_start(out=out[0:P, lo:hi], in_=total[0][:, lo:hi])
+        fetch(second[1], 1, pos2_sb, 1, 0, T)
+        add(0, 640, T)
         add(1, 0, 512)
         add(1, 512, T)

from contextlib import ExitStack

import concourse.mybir as mybir
from concourse.masks import make_identity

K, T, E, C, N = 1024, 768, 6, 256, 256
FLOPS = 2 * K * N * E * C
P = 128
PASSES = 2
BLOCKS = 2
SLOTS = E * C

F32 = mybir.dt.float32
BF16 = mybir.dt.bfloat16
U32 = mybir.dt.uint32
I32 = mybir.dt.int32
U16 = mybir.dt.uint16
U8 = mybir.dt.uint8
FP8X4 = mybir.dt.float8_e4m3fn_x4
MULT = mybir.AluOpType.mult
ADD = mybir.AluOpType.add
IDENTITY = mybir.ActivationFunctionType.Identity

CHUNKS = (((0, 256, 88), (256, 256, 88), (512, 128, 44), (640, 128, 44)), ((0, 256, 256), (256, 256, 256), (512, 256, 256)))
QUANT = (((0, 256), (256, 256), (512, 128), (640, 128)), ((0, 512), (512, 256)))
GATHER = 512


def interleave(copy, grouped, raw, lo, hi, base):
    if hi > lo:
        copy(
            grouped[:, lo + base : hi + base, :].rearrange("p (c i) t -> p c t i", i=4),
            raw[:, :, lo:hi].rearrange("p t (c i) -> p c t i", i=4),
        )


def tile_routed_moe_kernel(tc, xT, w_words, w_scales, b, gate, offs, pos1, pos2, out):
    nc = tc.nc
    with ExitStack() as ctx:
        keep = ctx.enter_context(tc.tile_pool(name="keep", bufs=1))
        psum = ctx.enter_context(tc.psum_pool(name="psum", bufs=8))

        offs_sb = keep.tile([P, SLOTS // 16], U16)
        pos1_sb = keep.tile([P, T // 16], U16)
        pos2_sb = keep.tile([P, T // 16], U16)
        bias = keep.tile([P, BLOCKS, E], F32)
        gates = keep.tile([P, 2, T], F32)
        w_codes = keep.tile([P, E, PASSES, 4 * N], U8, align_bytes=64)
        w_planes = keep.tile([P, E * PASSES, N], U8, align_bytes=64)
        x_planes = keep.tile([P, T], U8, align_bytes=64)
        s_planes = keep.tile([P, SLOTS], U8, align_bytes=64)
        s_codes = [keep.tile([P, SLOTS], U32, align_bytes=64, name=f"s_codes{a}") for a in range(PASSES)]
        y = [keep.tile([P, SLOTS], F32, name=f"y{n}") for n in range(BLOCKS)]

        nc.gpsimd.memset(x_planes[:], 0)
        ident = keep.tile([P, P], F32)
        make_identity(nc, ident[:])
        nc.vector.memset(w_planes[:].rearrange("p g n -> p (g n)").bitcast(I32), 0)

        x_rows = xT.rearrange("(a p t) n -> a p t n", p=P, t=4)
        raw = {}
        for a in range(PASSES):
            for lo, n, share in CHUNKS[a]:
                raw[a, lo] = keep.tile([P, 4, n], F32, name=f"raw{a}_{lo}")
                nc.sync.dma_start(out=raw[a, lo][:], in_=x_rows[a, :, :, lo : lo + n])
            if a == 0:
                nc.sync.dma_start(offs_sb[:], offs)
        for r in range(4):
            nc.sync.dma_start(
                out=w_planes[r : P : 32, :, :].bitcast(I32),
                in_=w_scales.rearrange("e a (q r) n -> r q (e a) n", r=4)[r].bitcast(I32),
            )
        for e in range(0, E, 2):
            nc.sync.dma_start(
                out=w_codes[:, e : e + 2, :, :].rearrange("p e a n -> p (e a) n"),
                in_=w_words[e : e + 2].rearrange("e a p n t -> p (e a) (n t)"),
            )
        nc.scalar.dma_start(out=bias[:], in_=b.rearrange("(c p) e -> p c e", p=P))
        nc.sync.dma_start(pos1_sb[:], pos1)
        nc.sync.dma_start(pos2_sb[:], pos2)
        nc.sync.dma_start(out=gates[:], in_=gate[:, 0:P, :].rearrange("g p n -> p g n"))

        def gather(slots, tokens, lo, hi):
            nc.vector.tensor_copy(slots[:, lo:hi], tokens[:].indirect(offs_sb[:, lo // 16 : hi // 16]))

        for a in range(PASSES):
            x_codes = keep.tile([P, T], U32, align_bytes=64, name=f"x_codes{a}")
            grouped = keep.tile([P, T, 4], BF16, align_bytes=64, name=f"grouped{a}")
            for lo, n, share in CHUNKS[a]:
                interleave(nc.scalar.copy, grouped, raw[a, lo], 0, share, lo)
                interleave(nc.vector.tensor_copy, grouped, raw[a, lo], share, n, lo)
            for lo, n in QUANT[a]:
                nc.vector.quantize_mx(
                    out=x_codes[:, lo : lo + n].bitcast(FP8X4),
                    scales=x_planes[4 * a : P, lo : lo + n],
                    in_=grouped[:, lo : lo + n, :].rearrange("p n t -> p (n t)"),
                )
            if a == 0:
                for s in range(0, SLOTS, GATHER):
                    gather(s_codes[0], x_codes, s, s + GATHER)

        def multiply(e):
            cols = slice(e * C, (e + 1) * C)
            accs = [psum.tile([P, 512], F32, name="acc") for n in range(BLOCKS)]
            for a in range(PASSES):
                for n in range(BLOCKS):
                    nc.tensor.matmul_mx(
                        out=accs[n][:, 0:C],
                        lhsT=w_codes[:, e, a, n * 512 : (n + 1) * 512].bitcast(FP8X4),
                        lhsT_scale=w_planes[:, e * PASSES + a, n * P : (n + 1) * P],
                        rhs=s_codes[a][:, cols].bitcast(FP8X4),
                        rhs_scale=s_planes[4 * a : P, cols],
                        start=(a == 0),
                        stop=(a == PASSES - 1),
                    )
            for n in range(BLOCKS):
                nc.scalar.activation(y[n][:, cols], accs[n][:, 0:C], IDENTITY, bias=bias[:, n, e : e + 1])

        for first in range(0, E, 2):
            lo, mid, hi = first * C, (first + 1) * C, (first + 2) * C
            gather(s_planes, x_planes, lo, hi)
            if first + 2 < E:
                gather(s_codes[1], x_codes, lo, hi)
            else:
                gather(s_codes[1], x_codes, lo, mid)
                gather(s_codes[1], x_codes, mid, hi)
            multiply(first)
            multiply(first + 1)

        def fetch(into, n, positions, weight, lo, hi):
            nc.vector.tensor_tensor(into[:, lo:hi], y[n][:].indirect(positions[:, lo // 16 : hi // 16]), gates[:, weight, lo:hi], MULT)

        first = [keep.tile([P, T], F32, name=f"first{n}") for n in range(BLOCKS)]
        second = [keep.tile([P, T], F32, name=f"second{n}") for n in range(BLOCKS)]
        total = [keep.tile([P, T], F32, name=f"total{n}") for n in range(BLOCKS)]
        pieces = ((0, 320), (320, 640))
        both = [psum.tile([P, 512], F32, name="acc") for piece in pieces]

        def add(n, lo, hi):
            nc.vector.tensor_tensor(total[n][:, lo:hi], first[n][:, lo:hi], second[n][:, lo:hi], ADD)
            nc.sync.dma_start(out=out[n * P : (n + 1) * P, lo:hi], in_=total[n][:, lo:hi])

        fetch(first[0], 0, pos1_sb, 0, 0, T)
        for acc, (lo, hi) in zip(both, pieces):
            nc.tensor.matmul(acc[:, 0 : hi - lo], ident[:], first[0][:, lo:hi], start=True, stop=False)
        fetch(second[0], 0, pos2_sb, 1, 0, T)
        for acc, (lo, hi) in zip(both, pieces):
            nc.tensor.matmul(acc[:, 0 : hi - lo], ident[:], second[0][:, lo:hi], start=False, stop=True)
        fetch(first[1], 1, pos1_sb, 0, 0, T)
        for acc, (lo, hi) in zip(both, pieces):
            nc.scalar.copy(total[0][:, lo:hi], acc[:, 0 : hi - lo])
            nc.sync.dma_start(out=out[0:P, lo:hi], in_=total[0][:, lo:hi])
        fetch(second[1], 1, pos2_sb, 1, 0, T)
        add(0, 640, T)
        add(1, 0, 512)
        add(1, 512, T)
